import numpy as np
import ml_dtypes


def mxq(x, axis, fmt="e4m3"):
    dtype, down = {"e4m3": (ml_dtypes.float8_e4m3fn, 7), "e5m2": (ml_dtypes.float8_e5m2, 14)}[fmt]
    v = np.moveaxis(np.asarray(x, np.float32).astype(ml_dtypes.bfloat16).astype(np.float64), axis, -1)
    blocks = v.reshape(v.shape[:-1] + (-1, 32))
    amax = np.abs(blocks).max(-1, keepdims=True)
    byte = np.maximum(np.where(amax > 0, np.frexp(amax)[1] - 1 + 127, 0) - down, 1)
    scale = np.exp2(byte - 127.0)
    codes = (blocks / scale).astype(np.float32).astype(dtype).astype(np.float64)
    return np.moveaxis((codes * scale).reshape(v.shape), -1, axis)


WIDE = False


def mx_kscale(k):
    if not WIDE:
        return np.ones(k)
    levels = np.array([10, -10, 5, -5, 0])
    if k % 512:
        return np.exp2(np.random.permutation(np.resize(levels, k // 32))).repeat(32)
    a = np.empty((k // 512, 16))
    for p in range(k // 512):
        a[p, :8] = np.random.permutation(np.resize(levels, 8))
        for g in range(8):
            far = levels[np.abs(levels - a[p, g]) >= 10]
            a[p, g + 8] = far[np.random.randint(len(far))]
    return np.exp2(a.ravel()).repeat(32)


BF16 = ml_dtypes.bfloat16


def bf(x):
    return np.asarray(x, np.float32).astype(BF16)


def f64(x):
    return np.asarray(x).astype(np.float64)


E2M1 = np.array([0.0, 0.5, 1.0, 1.5, 2.0, 3.0, 4.0, 6.0, -0.0, -0.5, -1.0, -1.5, -2.0, -3.0, -4.0, -6.0])


def pack_weight(w, fmt):
    k, n = w.shape
    w = f64(bf(w)).reshape(k // 32, 32, n)
    amax = np.abs(w).max(1)
    if fmt == "e4m3":
        byte = np.frexp(amax)[1] - 1 + 127 - 7
    else:
        mant, ex = np.frexp(amax / 6.0)
        byte = np.where(mant > 0.5, ex, ex - 1) + 127
    byte = np.clip(np.where(amax > 0, byte, 1), 1, 254)
    scaled = (w * np.exp2(127.0 - byte)[:, None, :]).reshape(k, n).astype(np.float32)
    by_word = np.ascontiguousarray(scaled.reshape(k // 512, 128, 4, n).transpose(0, 1, 3, 2))
    if fmt == "e4m3":
        words = by_word.astype(ml_dtypes.float8_e4m3fn).view(np.uint8)
    else:
        c = by_word.astype(ml_dtypes.float4_e2m1fn).view(np.uint8) & 0xF
        words = c[..., 0::2] | (c[..., 1::2] << 4)
    return np.ascontiguousarray(words), np.ascontiguousarray(byte.astype(np.uint8).reshape(k // 512, 16, n))


def unpack_weight(words, scales, fmt):
    g, p, n, _ = words.shape
    if fmt == "e4m3":
        vals = np.ascontiguousarray(words).view(ml_dtypes.float8_e4m3fn).astype(np.float64)
    else:
        nib = np.empty((g, p, n, 4), np.uint8)
        nib[..., 0::2] = words & 0xF
        nib[..., 1::2] = words >> 4
        vals = E2M1[nib]
    vals = vals * np.repeat(np.exp2(scales.astype(np.float64) - 127.0), 8, axis=1)[..., None]
    return vals.transpose(0, 1, 3, 2).reshape(g * 512, n)
def pack4(w):
    words, scales = pack_weight(w, "e2m1")
    return words.reshape(words.shape[0], 128, -1), scales


def unpack4(words, scales):
    return unpack_weight(words.reshape(words.shape[0], 128, -1, 2), scales, "e2m1")


M, D, V, R = 1024, 1024, 2048, 512


def draw0():
    s, t, r = mx_kscale(D), mx_kscale(V), mx_kscale(M)
    base = np.random.standard_normal((D, V))
    u_words, u_scales = pack4(base.T / np.sqrt(V) / t[:, None])
    return {"hid": bf(np.random.standard_normal((M, D)) * s),
            "w": bf(base / np.sqrt(D) / s[:, None]),
            "teach": bf(0.7 * np.random.standard_normal((M, V))),
            "centre": bf(0.3 * np.random.standard_normal(M)),
            "probs": bf(np.exp(0.5 * np.random.standard_normal((M, V))) * t * r[:, None]),
            "u_words": u_words, "u_scales": u_scales,
            "act": bf(np.random.standard_normal((M, R)) / np.sqrt(M) / r[:, None])}


def core(hid, w, teach, centre, probs, u_words, u_scales, act):
    z = mxq(f64(hid), 1, "e4m3") @ mxq(f64(w), 0, "e4m3")
    e = f64(probs) * (z - f64(teach) - f64(centre)[:, None])
    dhid = mxq(e, 1, "e4m3") @ unpack4(u_words, u_scales)
    dup = mxq(f64(act), 0, "e4m3").T @ mxq(e, 0, "e4m3")
    return dhid, dup


def e4m3fn_bytes(y):
    return np.clip(np.asarray(y, np.float64), -448.0, 448.0).astype(np.float32).astype(ml_dtypes.float8_e4m3fn).view(np.uint8)


def e4m3fn_values(b):
    return np.asarray(b, np.uint8).view(ml_dtypes.float8_e4m3fn).astype(np.float64)


def setup_inputs():
    d = draw0()
    x0 = np.asarray(d['w']).astype(np.float64)
    s = (np.max(np.abs(x0), axis=(1,), keepdims=True) / 448.0).astype(np.float32)
    out = {}
    for k, v in d.items():
        if k == 'w':
            out['w_bytes'] = e4m3fn_bytes(x0 / s.astype(np.float64))
            out['w_scale'] = s
        else:
            out[k] = v
    return out


def reference(hid, w_bytes, w_scale, teach, centre, probs, u_words, u_scales, act):
    return core(hid, e4m3fn_values(w_bytes) * w_scale.astype(np.float64), teach, centre, probs, u_words, u_scales, act)

from contextlib import ExitStack

import concourse.mybir as mybir
from concourse.masks import make_identity

F32 = mybir.dt.float32
BF16 = mybir.dt.bfloat16
U32 = mybir.dt.uint32
I32 = mybir.dt.int32
U8 = mybir.dt.uint8
FP8 = mybir.dt.float8_e4m3fn
FP8X4 = mybir.dt.float8_e4m3fn_x4
FP4X4 = mybir.dt.float4_e2m1fn_x4
ALU = mybir.AluOpType
ACT = mybir.ActivationFunctionType

M, D, V, R = 1024, 1024, 2048, 512
P = 128
C = 512
FLOPS = 2 * M * D * V * 2 + 2 * M * R * V


def tile_reverse_kl_backward_s8_kernel(
    tc, hid, w_bytes, w_scale, teach, centre, probs, u_words, u_scales, act, out_0, out_1
):
    nc = tc.nc
    with ExitStack() as ctx:
        keep = ctx.enter_context(tc.tile_pool(name="keep", bufs=1))
        work = ctx.enter_context(tc.tile_pool(name="work", bufs=2))
        psum = ctx.enter_context(tc.psum_pool(name="psum", bufs=1))
        ctx.enter_context(tc.manual_schedule())

        wsc = keep.tile([P, 8], F32, name="wsc")
        cen = keep.tile([P, 2, 4], BF16, name="cen")
        ident = keep.tile([P, P], F32, name="ident")
        hid_codes = keep.tile([P, 4, C], U32, name="hid_codes", align_bytes=64)
        hid_sc = keep.tile([P, 4, C], U8, name="hid_sc", align_bytes=64)
        w_codes = keep.tile([P, 2, V], U32, name="w_codes", align_bytes=64)
        w_sc = keep.tile([P, 2, V], U8, name="w_sc", align_bytes=64)
        e_codes = keep.tile([P, 2, V], U32, name="e_codes", align_bytes=64)
        e_sc = keep.tile([P, 2, V], U8, name="e_sc", align_bytes=64)
        et_codes = keep.tile([P, 8, C], U32, name="et_codes", align_bytes=64)
        et_sc = keep.tile([P, 8, C], U8, name="et_sc", align_bytes=64)
        act_codes = keep.tile([P, 2, R], U32, name="act_codes", align_bytes=64)
        act_sc = keep.tile([P, 2, R], U8, name="act_sc", align_bytes=64)
        u_codes = keep.tile([P, 4, 2 * D], U8, name="u_codes", align_bytes=64)
        u_sc = keep.tile([P, 4, D], U8, name="u_sc", align_bytes=64)

        nc.scalar.dma_start(out=wsc[:].rearrange("p (g t) -> p g t", t=4), in_=w_scale.rearrange("(g p t) o -> p g (t o)", p=P, t=4))
        nc.scalar.dma_start(out=cen[:], in_=centre.rearrange("(g p t) -> p g t", p=P, t=4))
        make_identity(nc, ident[:])
        nc.gpsimd.memset(u_sc[:].rearrange("p g n -> p (g n)").bitcast(I32), 0)

        w_view = w_bytes.rearrange("(g p t) v -> g p t v", p=P, t=4)
        wb_tiles = {}

        def load_w(kg, c, n=1):
            wb = work.tile([P, 4, n * C], U8, name="wb%d" % n, bufs=4 // n)
            nc.sync.dma_start(out=wb[:], in_=w_view[kg][:, :, c * C : (c + n) * C])
            for i in range(n):
                wb_tiles[kg, c + i] = wb[:, :, i * C : (i + 1) * C]

        rows = {}

        def load_hid(g, halves):
            hv = hid[g * C : (g + 1) * C, :].rearrange("(p t) d -> p t d", t=4)
            t = work.tile([P, 4, D], BF16, name="rows")
            for h in range(halves):
                n = 4 // halves
                nc.sync.dma_start(out=t[:, h * n : (h + 1) * n, :], in_=hv[:, h * n : (h + 1) * n, :])
            rows["hid", g] = t

        def load_act():
            t = work.tile([P, 4, D], BF16, name="rows")
            nc.sync.dma_start(
                out=t[:].rearrange("p a b -> p (a b)").rearrange("p (g x) -> p g x", g=2),
                in_=act.rearrange("(g p t) r -> p g (t r)", p=P, t=4),
            )
            rows["act"] = t

        tp = {}

        def load_tp(g, c):
            for nm, src in (("te", teach), ("pr", probs)):
                sv = src[g * C : (g + 1) * C, :].rearrange("(p t) v -> p t v", t=4)
                tp[nm, g, c] = work.tile([P, 4, C], BF16, name=nm, bufs=4)
                nc.sync.dma_start(out=tp[nm, g, c][:], in_=sv[:, :, c * C : (c + 1) * C])

        load_w(0, 0)
        load_hid(0, 2)
        load_w(1, 0)
        load_tp(0, 0)
        load_w(0, 1)
        load_w(1, 1)
        load_tp(0, 1)
        load_w(0, 2, 2)
        load_w(1, 2, 2)
        load_tp(0, 2)
        load_hid(1, 1)
        nc.sync.dma_start(out=u_codes[:], in_=u_words.rearrange("g p b -> p g b"))
        load_tp(0, 3)
        for q in range(4):
            nc.sync.dma_start(
                out=u_sc[32 * q : 32 * q + 4, :, :].bitcast(I32),
                in_=u_scales[:, 4 * q : 4 * q + 4, :].rearrange("g q n -> q g n").bitcast(I32),
            )
        load_act()
        load_tp(1, 0)
        load_tp(1, 1)
        load_tp(1, 2)
        load_tp(1, 3)

        wide = {}

        def widen(kg, c, engs):
            wide[kg, c] = work.tile([P, 4, C], BF16, name="wide", bufs=3)
            for t in range(4):
                src = wb_tiles[kg, c][:, t, :].bitcast(FP8)
                sc = wsc[:, 4 * kg + t : 4 * kg + t + 1]
                if engs[t] == "S":
                    nc.scalar.activation(out=wide[kg, c][:, t, :], in_=src, func=ACT.Copy, scale=sc)
                else:
                    nc.vector.tensor_scalar(out=wide[kg, c][:, t, :], in0=src, scalar1=sc, scalar2=None, op0=ALU.mult)

        ils = {}

        def il_tile(key, tag, bufs):
            ils[key] = work.tile([P, 4 * C], BF16, name=tag, align_bytes=64, bufs=bufs)

        def interleave(key, src, eng, a=0, b=C):
            s = src[:, :, a:b]
            o = ils[key][:, 4 * a : 4 * b]
            if eng == "G":
                nc.gpsimd.tensor_scalar(
                    out=o.rearrange("p (c t) -> p c t", t=4), in0=s.rearrange("p t c -> p c t"),
                    scalar1=1.0, scalar2=0.0, op0=ALU.mult, op1=ALU.add,
                )
                return
            o = o.rearrange("p (c i t) -> p c t i", i=4, t=4)
            s = s.rearrange("p t (c i) -> p c t i", i=4)
            if eng == "V":
                nc.vector.tensor_copy(out=o, in_=s)
            else:
                nc.scalar.copy(out=o, in_=s)

        def quant(key, codes, scales):
            nc.vector.quantize_mx(out=codes.bitcast(FP8X4), scales=scales, in_=ils[key][:])

        def turn(key, src, ts, bank, eng, at=0):
            b = psum.tile([P, 2, 2, P], F32, name=bank)
            for j, t in enumerate(ts):
                w = src[:, t, :].bitcast(F32)
                for u in range(2):
                    nc.tensor.transpose(b[:, j, u, :], w[:, u : 2 * P : 2], ident[:])
            n = len(ts)
            dst = ils[key][:].bitcast(F32).rearrange("q (t p u) -> q t p u", t=4, u=2)[:, ts[0] : ts[0] + n, :, :]
            s = b[:, 0:n, :, :].rearrange("q t u p -> q t p u")
            if eng == "S":
                nc.scalar.copy(out=dst, in_=s)
            else:
                nc.vector.tensor_copy(out=dst, in_=s)

        zb = {}

        def z_mm(n, t):
            g, c = units[n]
            zb[n, t] = psum.tile([P, C], F32, name="z%d" % ((4 * n + t) % 3))
            for kg in range(2):
                nc.tensor.matmul_mx(
                    out=zb[n, t][:],
                    lhsT=hid_codes[:, 2 * g + kg, t * P : (t + 1) * P].bitcast(FP8X4),
                    lhsT_scale=hid_sc[:, 2 * g + kg, t * P : (t + 1) * P],
                    rhs=w_codes[:, kg, c * C : (c + 1) * C].bitcast(FP8X4),
                    rhs_scale=w_sc[:, kg, c * C : (c + 1) * C],
                    start=kg == 0,
                    stop=kg == 1,
                )

        tmp = {}
        et = {}

        def stt(n, t):
            g, c = units[n]
            if t % 2 == 0:
                tmp[n, t // 2] = work.tile([P, 2, C], F32, name="tmp", bufs=3)
            nc.vector.scalar_tensor_tensor(
                out=tmp[n, t // 2][:, t % 2, :],
                in0=zb[n, t][:],
                scalar=cen[:, g, t : t + 1],
                in1=tp["te", g, c][:, t, :],
                op0=ALU.subtract,
                op1=ALU.subtract,
            )

        def tt(n, ts):
            g, c = units[n]
            if ts[0] == 0:
                et[n] = work.tile([P, 4, C], BF16, name="e")
            a, b = ts[0], ts[-1] + 1
            nc.vector.tensor_tensor(
                out=et[n][:, a:b, :],
                in0=tmp[n, a // 2][:, a % 2 : a % 2 + b - a, :],
                in1=tp["pr", g, c][:, a:b, :],
                op=ALU.mult,
            )

        def quant_tok(n):
            g, c = units[n]
            quant(("tok", n), e_codes[:, g, c * C : (c + 1) * C], e_sc[:, g, c * C : (c + 1) * C])

        def quant_voc(n, a=0, b=4):
            g, c = units[n]
            nc.vector.quantize_mx(
                out=et_codes[:, 4 * g + c, a * P : b * P].bitcast(FP8X4),
                scales=et_sc[:, 4 * g + c, a * P : b * P],
                in_=ils["voc", n][:, a * C : b * C],
            )

        def dhid_mm(bank, g, t, nh, cs):
            for c in cs:
                nc.tensor.matmul_mx(
                    out=bank[:],
                    lhsT=et_codes[:, 4 * g + c, t * P : (t + 1) * P].bitcast(FP8X4),
                    lhsT_scale=et_sc[:, 4 * g + c, t * P : (t + 1) * P],
                    rhs=u_codes[:, c, nh * 2 * C : (nh + 1) * 2 * C].bitcast(FP4X4),
                    rhs_scale=u_sc[:, c, nh * C : (nh + 1) * C],
                    start=c == 0,
                    stop=c == 3,
                )

        def copy_out(eng, bank, dst):
            r = work.tile([P, C], F32, name="res", bufs=6)
            if eng == "S":
                nc.scalar.copy(out=r[:], in_=bank[:])
            else:
                nc.vector.tensor_copy(out=r[:], in_=bank[:])
            nc.sync.dma_start(out=dst, in_=r[:])

        def dhid_out(eng, bank, g, t, nh):
            copy_out(eng, bank, out_0[g * C : (g + 1) * C, nh * C : (nh + 1) * C].rearrange("(p t) n -> p t n", t=4)[:, t, :])

        def dup(bank, r, c):
            for g in range(2):
                nc.tensor.matmul_mx(
                    out=bank[:],
                    lhsT=act_codes[:, g, r * P : (r + 1) * P].bitcast(FP8X4),
                    lhsT_scale=act_sc[:, g, r * P : (r + 1) * P],
                    rhs=e_codes[:, g, c * C : (c + 1) * C].bitcast(FP8X4),
                    rhs_scale=e_sc[:, g, c * C : (c + 1) * C],
                    start=g == 0,
                    stop=g == 1,
                )

        def dup_out(eng, bank, r, c):
            copy_out(eng, bank, out_1[r * P : (r + 1) * P, c * C : (c + 1) * C])

        def fbank(name):
            return psum.tile([P, C], F32, name=name)

        units = [(g, c) for g in range(2) for c in range(4)]
        G_COLS = 384

        def w_quant(kg, c):
            quant(("w", kg, c), w_codes[:, kg, c * C : (c + 1) * C], w_sc[:, kg, c * C : (c + 1) * C])

        def w_il(kg, c, eng):
            il_tile(("w", kg, c), "il_w", 2)
            interleave(("w", kg, c), wide[kg, c][:], eng)

        def hid_turn(g, kg, halves, banks):
            if 0 in halves:
                il_tile(("hid", g, kg), "il_t", 2)
            for h in halves:
                turn(("hid", g, kg), rows["hid", g][:, :, kg * C : (kg + 1) * C], (2 * h, 2 * h + 1), banks[h], "S")

        def hid_quant(g, kg):
            quant(("hid", g, kg), hid_codes[:, 2 * g + kg, :], hid_sc[:, 2 * g + kg, :])

        def act_rows(g):
            return rows["act"][:].rearrange("p a b -> p (a b)").rearrange("p (g t r) -> p g t r", g=2, t=4)[:, g, :, :]

        widen(0, 0, "VVSS")
        w_il(0, 0, "V")
        for h in range(2):
            for kg in range(2):
                hid_turn(0, kg, [h], {h: ("t0", "t1", "o0", "o1")[2 * h + kg]})
        w_quant(0, 0)
        widen(1, 0, "VVVS")
        hid_quant(0, 0)
        w_il(1, 0, "V")
        hid_quant(0, 1)
        w_quant(1, 0)
        widen(1, 1, "VVSS")
        widen(0, 1, "SSSS")
        for t in range(3):
            z_mm(0, t)

        dgroups = [(t, nh) for t in range(4) for nh in range(2)]
        held = {}
        ob = [0]

        def onext():
            ob[0] = (ob[0] + 1) % 3
            return fbank("o%d" % ob[0])

        def dhid_full(i, eng, g=0):
            t, nh = dgroups[i]
            b = onext()
            dhid_mm(b, g, t, nh, range(4))
            dhid_out(eng, b, g, t, nh)

        def dups(c, engs):
            for r in range(4):
                b = onext()
                dup(b, r, c)
                dup_out(engs[r], b, r, c)

        for n in range(8):
            g, c = units[n]
            stt(n, 0)
            z_mm(n, 3)
            for t in range(1, 4):
                stt(n, t)
                if g == 1 and n < 7:
                    z_mm(n + 1, t - 1)
            if n < 4:
                if c < 3:
                    w_il(0, c + 1, "V")
                    w_il(1, c + 1, "S")
                if n == 2:
                    hid_turn(1, 0, [0, 1], ("t0", "t1"))
                if n == 3:
                    hid_turn(1, 1, [0, 1], ("t0", "t1"))
                if n >= 1:
                    quant_voc(n - 1)
                    for i in range(3 if n >= 2 else 0):
                        if n == 2:
                            held[i] = fbank("o%d" % i)
                        dhid_mm(held[i], 0, *dgroups[i], [0, 1] if n == 2 else [2])
                if n == 3:
                    hid_quant(1, 0)
                    hid_quant(1, 1)
                    for g2 in range(2):
                        il_tile(("act", g2), "il_w", 2)
                        interleave(("act", g2), act_rows(g2), "S")
                if c < 3:
                    w_quant(0, c + 1)
                    w_quant(1, c + 1)
                    if c < 2:
                        widen(0, c + 2, "VSSS")
                        widen(1, c + 2, "SSSS")
                for t in range(3):
                    z_mm(n + 1, t)
            else:
                quant_voc(n - 1)
                if n == 4:
                    for i in range(3):
                        dhid_mm(held[i], 0, *dgroups[i], [3])
                        dhid_out("SVS"[i], held[i], 0, *dgroups[i])
                    dhid_full(3, "S")
                    dhid_full(4, "S")
                else:
                    dhid_full(n, "S")
                    quant_tok(n - 1)
                quant_tok(n - 4)
                if n == 4:
                    for g2 in range(2):
                        quant(("act", g2), act_codes[:, g2, :], act_sc[:, g2, :])
                else:
                    dups(units[n - 1][1], "SSSS")
            if n < 7:
                il_tile(("voc", n), "il_t", 2)
                il_tile(("tok", n), "il_e", 6)
                for h in range(2):
                    tt(n, (2 * h, 2 * h + 1))
                    turn(("voc", n), et[n][:], (2 * h, 2 * h + 1), "t%d" % h, "S")
                interleave(("tok", n), et[n][:], "G", 0, G_COLS)
                interleave(("tok", n), et[n][:], "S", G_COLS, C)

        n = 7
        il_tile(("voc", n), "il_t", 2)
        il_tile(("tok", n), "il_e", 6)
        held = {}
        for i in range(2):
            held[i] = fbank("z%d" % i)
            dhid_mm(held[i], 1, *dgroups[i], range(3))
        for t in range(4):
            tt(n, (t,))
            turn(("voc", n), et[n][:], (t,), "t%d" % (t % 2), "S")
            if t >= 1:
                quant_voc(n, t - 1, t)
        interleave(("tok", n), et[n][:], "V", 0, 320)
        interleave(("tok", n), et[n][:], "S", 320, C)
        quant_voc(n, 3, 4)
        quant_tok(n)
        for i in range(2, 6):
            held[i] = fbank("z2") if i == 2 else onext()
            dhid_mm(held[i], 1, *dgroups[i], range(3))
        for i in range(6):
            dhid_mm(held[i], 1, *dgroups[i], [3])
            dhid_out("VS"[i % 2], held[i], 1, *dgroups[i])
        for i in range(6, 8):
            b = fbank("t%d" % (i % 2))
            dhid_mm(b, 1, *dgroups[i], range(4))
            dhid_out("VS"[i % 2], b, 1, *dgroups[i])
        for r in range(4):
            b = fbank(("z0", "z1", "z2", "o0")[r])
            dup(b, r, 3)
            dup_out("VS"[r % 2], b, r, 3)
